import numpy as np
import ml_dtypes


def mxq(x, axis, fmt="e4m3"):
    dtype, down = {"e4m3": (ml_dtypes.float8_e4m3fn, 7), "e5m2": (ml_dtypes.float8_e5m2, 14)}[fmt]
    v = np.moveaxis(np.asarray(x, np.float32).astype(ml_dtypes.bfloat16).astype(np.float64), axis, -1)
    blocks = v.reshape(v.shape[:-1] + (-1, 32))
    amax = np.abs(blocks).max(-1, keepdims=True)
    byte = np.maximum(np.where(amax > 0, np.frexp(amax)[1] - 1 + 127, 0) - down, 1)
    scale = np.exp2(byte - 127.0)
    codes = (blocks / scale).astype(np.float32).astype(dtype).astype(np.float64)
    return np.moveaxis((codes * scale).reshape(v.shape), -1, axis)


WIDE = False


def mx_kscale(k):
    if not WIDE:
        return np.ones(k)
    levels = np.array([10, -10, 5, -5, 0])
    if k % 512:
        return np.exp2(np.random.permutation(np.resize(levels, k // 32))).repeat(32)
    a = np.empty((k // 512, 16))
    for p in range(k // 512):
        a[p, :8] = np.random.permutation(np.resize(levels, 8))
        for g in range(8):
            far = levels[np.abs(levels - a[p, g]) >= 10]
            a[p, g + 8] = far[np.random.randint(len(far))]
    return np.exp2(a.ravel()).repeat(32)


def f64(x):
    return np.asarray(x).astype(np.float64)


def striped(idx):
    return np.tile(idx.reshape(-1, 16).T, (8, 1)).astype(np.uint16)


def unstriped(offs):
    return offs[:16].T.reshape(-1).astype(np.int64)


E2M1 = np.array([0.0, 0.5, 1.0, 1.5, 2.0, 3.0, 4.0, 6.0, -0.0, -0.5, -1.0, -1.5, -2.0, -3.0, -4.0, -6.0])


def pack_weight(w, fmt):
    k, n = w.shape
    w = f64(np.asarray(w, np.float32).astype(ml_dtypes.bfloat16)).reshape(k // 32, 32, n)
    amax = np.abs(w).max(1)
    if fmt == "e4m3":
        byte = np.frexp(amax)[1] - 1 + 127 - 7
    else:
        mant, ex = np.frexp(amax / 6.0)
        byte = np.where(mant > 0.5, ex, ex - 1) + 127
    byte = np.clip(np.where(amax > 0, byte, 1), 1, 254)
    scaled = (w * np.exp2(127.0 - byte)[:, None, :]).reshape(k, n).astype(np.float32)
    by_word = np.ascontiguousarray(scaled.reshape(k // 512, 128, 4, n).transpose(0, 1, 3, 2))
    if fmt == "e4m3":
        words = by_word.astype(ml_dtypes.float8_e4m3fn).view(np.uint8)
    else:
        c = by_word.astype(ml_dtypes.float4_e2m1fn).view(np.uint8) & 0xF
        words = (c[..., 0::2] | (c[..., 1::2] << 4)).reshape(k // 512, 128, 2 * n)
    return np.ascontiguousarray(words), np.ascontiguousarray(byte.astype(np.uint8).reshape(k // 512, 16, n))


def unpack_weight(words, scales, fmt):
    g, _, n = scales.shape
    words = np.ascontiguousarray(words).reshape(g, 128, n, -1)
    if fmt == "e4m3":
        vals = words.view(ml_dtypes.float8_e4m3fn).astype(np.float64)
    else:
        nib = np.empty((g, 128, n, 4), np.uint8)
        nib[..., 0::2] = words & 0xF
        nib[..., 1::2] = words >> 4
        vals = E2M1[nib]
    vals = vals * np.repeat(np.exp2(scales.astype(np.float64) - 127.0), 8, axis=1)[..., None]
    return vals.transpose(0, 1, 3, 2).reshape(g * 512, n)


def planes(y):
    n, m = y.shape
    v = y.astype(np.float32).astype(ml_dtypes.bfloat16).astype(np.float64).reshape(n // 32, 32, m)
    top = np.abs(v).max(1)
    byte = np.clip(np.where(top > 0, np.frexp(top)[1] - 1 + 127 - 7, 1), 1, 254)
    codes = (v * np.exp2(127.0 - byte)[:, None, :]).reshape(n, m).astype(np.float32).astype(ml_dtypes.float8_e4m3fn).view(np.uint8)
    words = codes.reshape(n // 512, 128, 4, m).transpose(0, 1, 3, 2)
    return np.ascontiguousarray(words), np.ascontiguousarray(byte.astype(np.uint8).reshape(n // 512, 16, m))


def d_silu(v):
    s = 1.0 / (1.0 + np.exp(-np.maximum(v, -700.0)))
    return s * (1.0 + v * (1.0 - s))


K, T, E, C, H, N = 512, 1024, 3, 256, 512, 1024


def by_expert(wq, xq):
    return np.concatenate([wq[e].T @ xq[:, e * C:(e + 1) * C] for e in range(E)], axis=1)


def setup_inputs():
    n = np.random.standard_normal
    s = mx_kscale(K)
    v = mx_kscale(N)
    u = mx_kscale(H)
    slot_token = np.random.permutation(T)[:E * C]
    w_slot = np.random.uniform(0.2, 1.0, E * C)
    x = pack_weight(n((K, T)) * s[:, None], "e4m3")
    dy = pack_weight(n((N, T)) * v[:, None], "e4m3")
    m1 = n((E, K, H))
    w1 = [pack_weight(m, "e2m1") for m in m1 / np.sqrt(K) / s[None, :, None]]
    w2t = [pack_weight(m, "e2m1") for m in n((E, N, H)) / np.sqrt(N) / v[None, :, None] * u]
    w1t = [pack_weight(m, "e2m1") for m in m1.transpose(0, 2, 1) / np.sqrt(H) / u[None, :, None]]
    return {
        "x_words": x[0],
        "x_scales": x[1],
        "dy_words": dy[0],
        "dy_scales": dy[1],
        "w1_words": np.stack([m[0] for m in w1]),
        "w1_scales": np.stack([m[1] for m in w1]),
        "w2t_words": np.stack([m[0] for m in w2t]),
        "w2t_scales": np.stack([m[1] for m in w2t]),
        "w1t_words": np.stack([m[0] for m in w1t]),
        "w1t_scales": np.stack([m[1] for m in w1t]),
        "gate": (np.tile(w_slot, (128, 1))).astype(np.float32),
        "offs": striped(slot_token),
    }


def reference(x_words, x_scales, dy_words, dy_scales, w1_words, w1_scales, w2t_words, w2t_scales, w1t_words, w1t_scales, gate, offs):
    w1 = np.stack([unpack_weight(w1_words[e], w1_scales[e], "e2m1") for e in range(E)])
    w2t = np.stack([unpack_weight(w2t_words[e], w2t_scales[e], "e2m1") for e in range(E)])
    w1t = np.stack([unpack_weight(w1t_words[e], w1t_scales[e], "e2m1") for e in range(E)])
    idx = unstriped(offs)
    xq = unpack_weight(x_words, x_scales, "e4m3")[:, idx]
    gq = unpack_weight(dy_words, dy_scales, "e4m3")[:, idx]
    dh = f64(gate[:1]) * by_expert(w2t, gq)
    a = by_expert(w1, xq)
    dx = by_expert(w1t, mxq(dh * d_silu(a), 0, "e4m3"))
    out = np.zeros((K, T))
    out[:, idx] = dx
    out_0 = out
    return (out_0,) + planes(out_0)

@@ -1,0 +1,246 @@
+from contextlib import ExitStack
+
+import concourse.mybir as mybir
+from concourse.masks import make_identity
+
+K, T, E, C, H, N = 512, 1024, 3, 256, 512, 1024
+S = E * C
+P = 128
+BLOCKS = S // P
+FLOPS = 2 * S * (K * H + N * H + H * K)
+
+F32 = mybir.dt.float32
+BF16 = mybir.dt.bfloat16
+I32 = mybir.dt.int32
+U32 = mybir.dt.uint32
+U16 = mybir.dt.uint16
+U8 = mybir.dt.uint8
+FP8X4 = mybir.dt.float8_e4m3fn_x4
+FP4X4 = mybir.dt.float4_e2m1fn_x4
+ALU = mybir.AluOpType
+ACT = mybir.ActivationFunctionType
+
+
+def tile_moe_rec_mlp_silu_kernel(
+    tc, x_words, x_scales, dy_words, dy_scales, w1_words, w1_scales, w2t_words, w2t_scales,
+    w1t_words, w1t_scales, gate, offs, out_0, out_1, out_2,
+):
+    nc = tc.nc
+    with ExitStack() as ctx:
+        keep = ctx.enter_context(tc.tile_pool(name="keep", bufs=1))
+        work = ctx.enter_context(tc.tile_pool(name="work", bufs=3))
+        psum = ctx.enter_context(tc.psum_pool(name="psum", bufs=2))
+
+        def held(shape, dtype, name):
+            return keep.tile(shape, dtype, name=name, align_bytes=64)
+
+        offsets = keep.tile([P, S // 16], U16, name="offsets")
+        x_win = held([P, T], I32, "x_win")
+        dy_win = [held([P, T], I32, f"dy_win{s}") for s in range(2)]
+        xs_win = held([P, T], U8, "xs_win")
+        dys_win = held([P, 2 * T], U8, "dys_win")
+        w1_sc = held([P, E * H], U8, "w1_sc")
+        w2_sc = held([P, E * 2 * H], U8, "w2_sc")
+        w1t_sc_raw = held([P, E * K], U8, "w1t_sc_raw")
+        w1_first = held([P, 2 * H], U8, "w1_first")
+        w1_rest = held([P, (E - 1) * 2 * H], U8, "w1_rest")
+        w2_first = held([P, 2 * 2 * H], U8, "w2_first")
+        w2_rest = held([P, (E - 1) * 2 * 2 * H], U8, "w2_rest")
+        w1t_first = held([P, 2 * K], U8, "w1t_first")
+        w1t_rest = held([P, (E - 1) * 2 * K], U8, "w1t_rest")
+        g_rows = keep.tile([P, P], F32, name="g_rows")
+        g_neg = keep.tile([P, BLOCKS], F32, name="g_neg")
+        ident = keep.tile([P, P], F32, name="ident")
+
+        for plane in (xs_win, dys_win):
+            nc.gpsimd.memset(plane[:].bitcast(I32), 0)
+        make_identity(nc, ident[:])
+        nc.gpsimd.memset(w1t_sc_raw[:].bitcast(I32), 0)
+
+        def load_scales(plane, rows, n):
+            for q in range(4):
+                nc.sync.dma_start(
+                    out=plane[32 * q:32 * q + 4, :].bitcast(I32).rearrange("r (g w) -> r g w", g=n),
+                    in_=rows[:, 4 * q:4 * q + 4, :].bitcast(I32).rearrange("g r w -> r g w"),
+                )
+
+        def load_words(tile, words, n):
+            nc.sync.dma_start(
+                out=tile[:].bitcast(I32).rearrange("p (g w) -> p g w", g=n),
+                in_=words.bitcast(I32).rearrange("g p w -> p g w"),
+            )
+
+        w1_w = w1_words.rearrange("e s p c -> (e s) p c")
+        w2_w = w2t_words.rearrange("e s p c -> (e s) p c")
+        w1t_w = w1t_words.rearrange("e s p c -> (e s) p c")
+
+        nc.sync.dma_start(offsets[:], offs)
+        nc.sync.dma_start(out=x_win[:], in_=x_words[0].rearrange("p t d -> p (t d)").bitcast(I32))
+        load_scales(xs_win, x_scales, 1)
+        for s in range(2):
+            nc.sync.dma_start(out=dy_win[s][:], in_=dy_words[s].rearrange("p t d -> p (t d)").bitcast(I32))
+        load_scales(dys_win, dy_scales, 2)
+        load_words(w1_first, w1_w[0:1], 1)
+        load_scales(w1_sc, w1_scales.rearrange("e s b i -> (e s) b i"), E)
+        load_words(w2_first, w2_w[0:2], 2)
+        load_scales(w2_sc, w2t_scales.rearrange("e s b i -> (e s) b i"), 2 * E)
+        nc.sync.dma_start(out=g_rows[:], in_=gate.rearrange("r (b j) -> (r b) j", j=P)[0:P, :])
+        load_words(w1t_first, w1t_w[0:1], 1)
+        load_scales(w1t_sc_raw, w1t_scales.rearrange("e s b i -> (e s) b i"), E)
+        load_words(w1_rest, w1_w[1:E], E - 1)
+        load_words(w2_rest, w2_w[2:2 * E], 2 * (E - 1))
+        load_words(w1t_rest, w1t_w[1:E], E - 1)
+
+        out_win = [held([P, T], F32, f"out_win{t}") for t in range(4)]
+        for t in range(4):
+            nc.vector.memset(out_win[t][:], 0.0)
+
+        g_turned = psum.tile([P, 2, P], F32, name="turned")
+        nc.tensor.transpose(g_turned[:, 0, :], g_rows[:], ident[:])
+        nc.scalar.activation(out=g_neg[:], in_=g_turned[:, 0, 0:BLOCKS], func=ACT.Copy, scale=-1.0)
+
+        def expert_words(first, rest, e, width):
+            if e == 0:
+                return first[:, 0:width]
+            return rest[:, (e - 1) * width:e * width]
+
+        w1t_perm = [held([P, 2 * K], U8, f"w1t_perm{e}") for e in range(E)]
+        w1t_sc = [held([P, K], U8, f"w1t_sc{e}") for e in range(E)]
+
+        def deal_w1t(e):
+            nc.scalar.copy(
+                out=w1t_perm[e][:].bitcast(U16).rearrange("p (t m) -> p t m", t=4),
+                in_=expert_words(w1t_first, w1t_rest, e, 2 * K).bitcast(U16).rearrange("p (m t) -> p t m", t=4),
+            )
+            nc.vector.tensor_copy(
+                out=w1t_sc[e][:].rearrange("p (t m) -> p t m", t=4),
+                in_=w1t_sc_raw[:, e * K:(e + 1) * K].rearrange("p (m t) -> p t m", t=4),
+            )
+
+        def listed(lo, hi):
+            return offsets[:, lo // 16:hi // 16]
+
+        def gather(b):
+            slots = listed(b * P, (b + 1) * P)
+            x_g = work.tile([P, P], U32, name="x_g", align_bytes=64)
+            xs_g = work.tile([P, P], U8, name="xs_g", align_bytes=64)
+            nc.vector.tensor_copy(x_g[:], x_win[:].bitcast(U32).indirect(slots))
+            nc.vector.tensor_copy(xs_g[:], xs_win[:].indirect(slots))
+            dy_g = [work.tile([P, P], U32, name=f"dy_g{s}", align_bytes=64) for s in range(2)]
+            dys_g = [work.tile([P, P], U8, name=f"dys_g{s}", align_bytes=64) for s in range(2)]
+            for s in range(2):
+                nc.vector.tensor_copy(dy_g[s][:], dy_win[s][:].bitcast(U32).indirect(slots))
+                nc.vector.tensor_copy(dys_g[s][:], dys_win[:, s * T:(s + 1) * T].indirect(slots))
+            return x_g, xs_g, dy_g, dys_g
+
+        dx = held([P, 4, S], F32, "dx")
+
+        def first_stage(b, x_g, xs_g, dy_g, dys_g):
+            e = b * P // C
+            a_ps = psum.tile([P, H], F32, name="a_ps")
+            nc.tensor.matmul_mx(
+                out=a_ps[:], lhsT=x_g[:].bitcast(FP8X4), lhsT_scale=xs_g[:],
+                rhs=expert_words(w1_first, w1_rest, e, 2 * H).bitcast(FP4X4),
+                rhs_scale=w1_sc[:, e * H:(e + 1) * H], start=True, stop=True,
+            )
+            dh_ps = psum.tile([P, H], F32, name="dh_ps")
+            w2_e = expert_words(w2_first, w2_rest, e, 4 * H)
+            for s in range(2):
+                nc.tensor.matmul_mx(
+                    out=dh_ps[:], lhsT=dy_g[s][:].bitcast(FP8X4), lhsT_scale=dys_g[s][:],
+                    rhs=w2_e[:, s * 2 * H:(s + 1) * 2 * H].bitcast(FP4X4),
+                    rhs_scale=w2_sc[:, (2 * e + s) * H:(2 * e + s + 1) * H], start=(s == 0), stop=(s == 1),
+                )
+            m = work.tile([P, H], F32, name="m")
+            nc.scalar.activation(out=m[:], in_=a_ps[:], func=ACT.Sigmoid, scale=-1.0)
+            ng = g_neg[:, b:b + 1]
+            u = work.tile([P, H], F32, name="u")
+            nc.vector.scalar_tensor_tensor(u[:], a_ps[:], ng, m[:], ALU.mult, ALU.mult)
+            v = work.tile([P, H], F32, name="v")
+            nc.vector.scalar_tensor_tensor(v[:], u[:], ng, dh_ps[:], ALU.add, ALU.mult)
+            da = work.tile([P, H], BF16, name="da", align_bytes=64)
+            nc.vector.scalar_tensor_tensor(da[:], m[:], 1.0, v[:], ALU.subtract, ALU.mult)
+            return da
+
+        def second_stage(b, da):
+            e = b * P // C
+            cols = slice(b * P, (b + 1) * P)
+            pairs = da[:].bitcast(F32)
+            turned = psum.tile([P, 2, P], F32, name="turned")
+            for h in range(2):
+                nc.tensor.transpose(turned[:, h, :], pairs[:, h:H // 2:2], ident[:])
+            da_t = work.tile([P, P * 4], BF16, name="da_t", align_bytes=64)
+            nc.vector.tensor_copy(
+                out=da_t[:].bitcast(F32).rearrange("p (j h) -> p j h", h=2),
+                in_=turned[:].rearrange("p h j -> p j h"),
+            )
+            codes = work.tile([P, P], U32, name="codes", align_bytes=64)
+            scales = work.tile([P, P], U8, name="scales", align_bytes=64)
+            nc.vector.quantize_mx(out=codes[:].bitcast(FP8X4), scales=scales[:], in_=da_t[:])
+            dx_ps = psum.tile([P, 4, P], F32, name="dx_ps")
+            for t in range(4):
+                nc.tensor.matmul_mx(
+                    out=dx_ps[:, t, :], lhsT=w1t_perm[e][:, 2 * P * t:2 * P * (t + 1)].bitcast(FP4X4),
+                    lhsT_scale=w1t_sc[e][:, P * t:P * (t + 1)],
+                    rhs=codes[:].bitcast(FP8X4), rhs_scale=scales[:], start=True, stop=True,
+                )
+            nc.scalar.copy(out=dx[:, :, cols], in_=dx_ps[:])
+
+        def scatter_scalar(t, lo, hi):
+            nc.scalar.activation(out=out_win[t][:].indirect(listed(lo, hi)), in_=dx[:, t, lo:hi], func=ACT.Copy)
+
+        def scatter_vector(t, lo, hi):
+            nc.vector.tensor_copy(out_win[t][:].indirect(listed(lo, hi)), dx[:, t, lo:hi])
+
+        def scatter_block(b):
+            lo, hi = b * P, (b + 1) * P
+            if b < BLOCKS // 2:
+                for t in range(4):
+                    scatter_scalar(t, lo, hi)
+            else:
+                scatter_scalar(0, lo, hi)
+                scatter_vector(1, lo, hi)
+
+        gathered = [gather(0), gather(1)]
+        pending = None
+        for b in range(BLOCKS):
+            if b % 2 == 0:
+                deal_w1t(b // 2)
+            da = first_stage(b, *gathered[b])
+            if b + 2 < BLOCKS:
+                gathered.append(gather(b + 2))
+            if pending is not None:
+                second_stage(*pending)
+                scatter_block(pending[0])
+            pending = (b, da)
+        second_stage(*pending)
+        scatter_block(BLOCKS - 1)
+        scatter_scalar(2, S // 2, S)
+        scatter_vector(3, S // 2, S)
+
+        rows = out_0.rearrange("(p t) n -> p t n", t=4)
+        planes = held([P, 4, T], BF16, "planes")
+        for t in range(4):
+            nc.sync.dma_start(out=rows[:, t, :], in_=out_win[t][:])
+            if t == 2:
+                nc.scalar.copy(out=planes[:, t, :], in_=out_win[t][:])
+            else:
+                nc.vector.tensor_copy(out=planes[:, t, :], in_=out_win[t][:])
+
+        y_scales = held([P, T], U8, "y_scales")
+        words_out = out_1[0].rearrange("p t d -> p (t d)").bitcast(I32)
+        for lo, hi, engine in ((0, 384, "scalar"), (384, 512, "vector"), (512, 1024, "vector")):
+            woven = held([P, (hi - lo) * 4], BF16, f"woven{lo}")
+            src = planes[:, :, lo:hi].rearrange("p t n -> p n t")
+            dst = woven[:].rearrange("p (n t) -> p n t", t=4)
+            if engine == "scalar":
+                nc.scalar.copy(out=dst, in_=src)
+            else:
+                nc.vector.tensor_copy(out=dst, in_=src)
+            y_codes = held([P, hi - lo], I32, f"y_codes{lo}")
+            nc.vector.quantize_mx(out=y_codes[:].bitcast(FP8X4), scales=y_scales[:, lo:hi], in_=woven[:])
+            nc.sync.dma_start(out=words_out[:, lo:hi], in_=y_codes[:])
+        for q in range(4):
+            nc.sync.dma_start(
+                out=out_2[0, 4 * q:4 * q + 4, :].bitcast(I32), in_=y_scales[32 * q:32 * q + 4, :].bitcast(I32)
+            )

@@ -20,6 +20,8 @@ FP4X4 = mybir.dt.float4_e2m1fn_x4
 ALU = mybir.AluOpType
 ACT = mybir.ActivationFunctionType
 
+SLOT = {"w1t_perm0":"xs_g0","w1t_perm1":"da_t0","w1t_sc0":"v0","dy_g0_256":"dys_g0_0","dys_g0_256":"dys_g0_128","dy_g1_256":"dys_g1_0","dys_g1_256":"dys_g1_128","w1t_sc1":"da_t1","dy_g0_512":"scales1","dys_g0_512":"codes1","dy_g1_512":"v2","dys_g1_512":"da2","out_win3":"out_win3"}
+
 
 def tile_moe_rec_mlp_silu_kernel(
     tc, x_words, x_scales, dy_words, dy_scales, w1_words, w1_scales, w2t_words, w2t_scales,
@@ -28,22 +30,20 @@ def tile_moe_rec_mlp_silu_kernel(
     nc = tc.nc
     with ExitStack() as ctx:
         keep = ctx.enter_context(tc.tile_pool(name="keep", bufs=1))
-        work = ctx.enter_context(tc.tile_pool(name="work", bufs=3))
         psum = ctx.enter_context(tc.psum_pool(name="psum", bufs=2))
 
         def held(shape, dtype, name):
-            return keep.tile(shape, dtype, name=name, align_bytes=64)
+            return keep.tile(shape, dtype, name=name, tag=SLOT.get(name, name), align_bytes=64)
 
         offsets = keep.tile([P, S // 16], U16, name="offsets")
         x_win = held([P, T], I32, "x_win")
-        dy_win = [held([P, T], I32, f"dy_win{s}") for s in range(2)]
+        dy_win = held([P, 2 * T], I32, "dy_win")
         xs_win = held([P, T], U8, "xs_win")
         dys_win = held([P, 2 * T], U8, "dys_win")
         w1_sc = held([P, E * H], U8, "w1_sc")
         w2_sc = held([P, E * 2 * H], U8, "w2_sc")
         w1t_sc_raw = held([P, E * K], U8, "w1t_sc_raw")
-        w1_first = held([P, 2 * H], U8, "w1_first")
-        w1_rest = held([P, (E - 1) * 2 * H], U8, "w1_rest")
+        w1_all = held([P, E * 2 * H], U8, "w1_all")
         w2_first = held([P, 2 * 2 * H], U8, "w2_first")
         w2_rest = held([P, (E - 1) * 2 * 2 * H], U8, "w2_rest")
         w1t_first = held([P, 2 * K], U8, "w1t_first")
@@ -57,9 +57,9 @@ def tile_moe_rec_mlp_silu_kernel(
         make_identity(nc, ident[:])
         nc.gpsimd.memset(w1t_sc_raw[:].bitcast(I32), 0)
 
-        def load_scales(plane, rows, n):
-            for q in range(4):
-                nc.sync.dma_start(
+        def load_scales(plane, rows, n, quadrants=range(4), queue=nc.sync):
+            for q in quadrants:
+                queue.dma_start(
                     out=plane[32 * q:32 * q + 4, :].bitcast(I32).rearrange("r (g w) -> r g w", g=n),
                     in_=rows[:, 4 * q:4 * q + 4, :].bitcast(I32).rearrange("g r w -> r g w"),
                 )
@@ -77,106 +77,137 @@ def tile_moe_rec_mlp_silu_kernel(
         nc.sync.dma_start(offsets[:], offs)
         nc.sync.dma_start(out=x_win[:], in_=x_words[0].rearrange("p t d -> p (t d)").bitcast(I32))
         load_scales(xs_win, x_scales, 1)
-        for s in range(2):
-            nc.sync.dma_start(out=dy_win[s][:], in_=dy_words[s].rearrange("p t d -> p (t d)").bitcast(I32))
-        load_scales(dys_win, dy_scales, 2)
-        load_words(w1_first, w1_w[0:1], 1)
+        load_words(dy_win, dy_words.rearrange("s p t d -> s p (t d)"), 2)
+        load_words(w1_all, w1_w, E)
+        nc.sync.dma_start(out=g_rows[:], in_=gate.rearrange("r (b j) -> (r b) j", j=P)[0:P, :])
         load_scales(w1_sc, w1_scales.rearrange("e s b i -> (e s) b i"), E)
+        load_scales(dys_win, dy_scales, 2)
         load_words(w2_first, w2_w[0:2], 2)
         load_scales(w2_sc, w2t_scales.rearrange("e s b i -> (e s) b i"), 2 * E)
-        nc.sync.dma_start(out=g_rows[:], in_=gate.rearrange("r (b j) -> (r b) j", j=P)[0:P, :])
         load_words(w1t_first, w1t_w[0:1], 1)
         load_scales(w1t_sc_raw, w1t_scales.rearrange("e s b i -> (e s) b i"), E)
-        load_words(w1_rest, w1_w[1:E], E - 1)
         load_words(w2_rest, w2_w[2:2 * E], 2 * (E - 1))
         load_words(w1t_rest, w1t_w[1:E], E - 1)
 
         out_win = [held([P, T], F32, f"out_win{t}") for t in range(4)]
-        for t in range(4):
+        for t in range(3):
             nc.vector.memset(out_win[t][:], 0.0)
+        nc.gpsimd.memset(out_win[3][:], 0.0)
 
         g_turned = psum.tile([P, 2, P], F32, name="turned")
         nc.tensor.transpose(g_turned[:, 0, :], g_rows[:], ident[:])
-        nc.scalar.activation(out=g_neg[:], in_=g_turned[:, 0, 0:BLOCKS], func=ACT.Copy, scale=-1.0)
+        nc.scalar.activation(out=g_neg[:], in_=g_turned[:, 0, 0:BLOCKS], func=ACT.Copy, scale=-0.5)
 
         def expert_words(first, rest, e, width):
             if e == 0:
                 return first[:, 0:width]
             return rest[:, (e - 1) * width:e * width]
 
-        w1t_perm = [held([P, 2 * K], U8, f"w1t_perm{e}") for e in range(E)]
-        w1t_sc = [held([P, K], U8, f"w1t_sc{e}") for e in range(E)]
-
-        def deal_w1t(e):
-            nc.scalar.copy(
-                out=w1t_perm[e][:].bitcast(U16).rearrange("p (t m) -> p t m", t=4),
-                in_=expert_words(w1t_first, w1t_rest, e, 2 * K).bitcast(U16).rearrange("p (m t) -> p t m", t=4),
-            )
-            nc.vector.tensor_copy(
-                out=w1t_sc[e][:].rearrange("p (t m) -> p t m", t=4),
-                in_=w1t_sc_raw[:, e * K:(e + 1) * K].rearrange("p (m t) -> p t m", t=4),
-            )
-
         def listed(lo, hi):
             return offsets[:, lo // 16:hi // 16]
 
-        def gather(b):
-            slots = listed(b * P, (b + 1) * P)
-            x_g = work.tile([P, P], U32, name="x_g", align_bytes=64)
-            xs_g = work.tile([P, P], U8, name="xs_g", align_bytes=64)
+        w1t_perm, w1t_sc = {}, {}
+
+        def deal_words(words, first, last):
+            n = last - first
+            dealt = held([P, n * 2 * K], U8, f"w1t_perm{first}")
+            nc.scalar.copy(
+                out=dealt[:].bitcast(U16).rearrange("p (e t m) -> p e t m", e=n, t=4),
+                in_=words[:].bitcast(U16).rearrange("p (e m t) -> p e t m", e=n, t=4),
+            )
+            for e in range(first, last):
+                w1t_perm[e] = dealt[:, (e - first) * 2 * K:(e - first + 1) * 2 * K]
+
+        def deal_scales(first, last):
+            n = last - first
+            dealt = held([P, n * K], U8, f"w1t_sc{first}")
+            nc.vector.tensor_copy(
+                out=dealt[:].rearrange("p (e t m) -> p e t m", e=n, t=4),
+                in_=w1t_sc_raw[:, first * K:last * K].rearrange("p (e m t) -> p e t m", e=n, t=4),
+            )
+            for e in range(first, last):
+                w1t_sc[e] = dealt[:, (e - first) * K:(e - first + 1) * K]
+
+        x_of, dy_of = {}, {}
+
+        def gather_x(lo, hi):
+            slots = listed(lo, hi)
+            x_g = held([P, hi - lo], U32, f"x_g{lo}")
+            xs_g = held([P, hi - lo], U8, f"xs_g{lo}")
             nc.vector.tensor_copy(x_g[:], x_win[:].bitcast(U32).indirect(slots))
             nc.vector.tensor_copy(xs_g[:], xs_win[:].indirect(slots))
-            dy_g = [work.tile([P, P], U32, name=f"dy_g{s}", align_bytes=64) for s in range(2)]
-            dys_g = [work.tile([P, P], U8, name=f"dys_g{s}", align_bytes=64) for s in range(2)]
+            for b in range(lo // P, hi // P):
+                cols = slice(b * P - lo, (b + 1) * P - lo)
+                x_of[b] = (x_g[:, cols], xs_g[:, cols])
+
+        def gather_dy(lo, hi):
+            n = hi - lo
+            slots = listed(lo, hi)
+            dy_g = [held([P, n], U32, f"dy_g{s}_{lo}") for s in range(2)]
+            dys_g = [held([P, n], U8, f"dys_g{s}_{lo}") for s in range(2)]
             for s in range(2):
-                nc.vector.tensor_copy(dy_g[s][:], dy_win[s][:].bitcast(U32).indirect(slots))
+                nc.vector.tensor_copy(dy_g[s][:], dy_win[:, s * T:(s + 1) * T].bitcast(U32).indirect(slots))
                 nc.vector.tensor_copy(dys_g[s][:], dys_win[:, s * T:(s + 1) * T].indirect(slots))
-            return x_g, xs_g, dy_g, dys_g
+            for b in range(lo // P, hi // P):
+                cols = slice(b * P - lo, (b + 1) * P - lo)
+                dy_of[b] = ([g[:, cols] for g in dy_g], [g[:, cols] for g in dys_g])
 
         dx = held([P, 4, S], F32, "dx")
+        n_of, sg_of = {}, {}
 
-        def first_stage(b, x_g, xs_g, dy_g, dys_g):
+        def token_side(b):
             e = b * P // C
+            x_g, xs_g = x_of[b]
             a_ps = psum.tile([P, H], F32, name="a_ps")
             nc.tensor.matmul_mx(
-                out=a_ps[:], lhsT=x_g[:].bitcast(FP8X4), lhsT_scale=xs_g[:],
-                rhs=expert_words(w1_first, w1_rest, e, 2 * H).bitcast(FP4X4),
+                out=a_ps[:], lhsT=x_g.bitcast(FP8X4), lhsT_scale=xs_g,
+                rhs=w1_all[:, e * 2 * H:(e + 1) * 2 * H].bitcast(FP4X4),
                 rhs_scale=w1_sc[:, e * H:(e + 1) * H], start=True, stop=True,
             )
+            n = held([P, H], F32, f"n{b}")
+            nc.scalar.activation(out=n[:], in_=a_ps[:], func=ACT.Silu, scale=-1.0)
+            th = held([P, H], F32, f"th{b}")
+            nc.scalar.activation(out=th[:], in_=a_ps[:], func=ACT.Tanh, scale=0.5)
+            sg = held([P, H], F32, f"sg{b}")
+            nc.gpsimd.tensor_scalar(sg[:], th[:], g_neg[:, b:b + 1], g_neg[:, b:b + 1], ALU.mult, ALU.add)
+            n_of[b], sg_of[b] = n, sg
+
+        def gradient_side(b):
+            e = b * P // C
+            dy_g, dys_g = dy_of[b]
             dh_ps = psum.tile([P, H], F32, name="dh_ps")
             w2_e = expert_words(w2_first, w2_rest, e, 4 * H)
             for s in range(2):
                 nc.tensor.matmul_mx(
-                    out=dh_ps[:], lhsT=dy_g[s][:].bitcast(FP8X4), lhsT_scale=dys_g[s][:],
+                    out=dh_ps[:], lhsT=dy_g[s].bitcast(FP8X4), lhsT_scale=dys_g[s],
                     rhs=w2_e[:, s * 2 * H:(s + 1) * 2 * H].bitcast(FP4X4),
                     rhs_scale=w2_sc[:, (2 * e + s) * H:(2 * e + s + 1) * H], start=(s == 0), stop=(s == 1),
                 )
-            m = work.tile([P, H], F32, name="m")
-            nc.scalar.activation(out=m[:], in_=a_ps[:], func=ACT.Sigmoid, scale=-1.0)
-            ng = g_neg[:, b:b + 1]
-            u = work.tile([P, H], F32, name="u")
-            nc.vector.scalar_tensor_tensor(u[:], a_ps[:], ng, m[:], ALU.mult, ALU.mult)
-            v = work.tile([P, H], F32, name="v")
-            nc.vector.scalar_tensor_tensor(v[:], u[:], ng, dh_ps[:], ALU.add, ALU.mult)
-            da = work.tile([P, H], BF16, name="da", align_bytes=64)
-            nc.vector.scalar_tensor_tensor(da[:], m[:], 1.0, v[:], ALU.subtract, ALU.mult)
+            v = held([P, H], F32, f"v{b}")
+            nc.vector.scalar_tensor_tensor(v[:], n_of[b][:], 1.0, dh_ps[:], ALU.subtract, ALU.mult)
+            da = held([P, H], BF16, f"da{b}")
+            nc.vector.tensor_tensor(da[:], v[:], sg_of[b][:], ALU.mult)
             return da
 
-        def second_stage(b, da):
-            e = b * P // C
-            cols = slice(b * P, (b + 1) * P)
+        def turn(b, da):
             pairs = da[:].bitcast(F32)
             turned = psum.tile([P, 2, P], F32, name="turned")
             for h in range(2):
                 nc.tensor.transpose(turned[:, h, :], pairs[:, h:H // 2:2], ident[:])
-            da_t = work.tile([P, P * 4], BF16, name="da_t", align_bytes=64)
-            nc.vector.tensor_copy(
+            da_t = held([P, P * 4], BF16, f"da_t{b}")
+            weave_pairs = nc.scalar.copy if b == 0 else nc.vector.tensor_copy
+            weave_pairs(
                 out=da_t[:].bitcast(F32).rearrange("p (j h) -> p j h", h=2),
                 in_=turned[:].rearrange("p h j -> p j h"),
             )
-            codes = work.tile([P, P], U32, name="codes", align_bytes=64)
-            scales = work.tile([P, P], U8, name="scales", align_bytes=64)
+            codes = held([P, P], U32, f"codes{b}")
+            scales = held([P, P], U8, f"scales{b}")
             nc.vector.quantize_mx(out=codes[:].bitcast(FP8X4), scales=scales[:], in_=da_t[:])
+            return codes, scales
+
+        def second_stage(b, codes, scales):
+            e = b * P // C
+            cols = slice(b * P, (b + 1) * P)
             dx_ps = psum.tile([P, 4, P], F32, name="dx_ps")
             for t in range(4):
                 nc.tensor.matmul_mx(
@@ -184,7 +215,8 @@ def tile_moe_rec_mlp_silu_kernel(
                     lhsT_scale=w1t_sc[e][:, P * t:P * (t + 1)],
                     rhs=codes[:].bitcast(FP8X4), rhs_scale=scales[:], start=True, stop=True,
                 )
-            nc.scalar.copy(out=dx[:, :, cols], in_=dx_ps[:])
+            empty = nc.scalar.copy if b < 3 else nc.vector.tensor_copy
+            empty(out=dx[:, :, cols], in_=dx_ps[:])
 
         def scatter_scalar(t, lo, hi):
             nc.scalar.activation(out=out_win[t][:].indirect(listed(lo, hi)), in_=dx[:, t, lo:hi], func=ACT.Copy)
@@ -192,38 +224,45 @@ def tile_moe_rec_mlp_silu_kernel(
         def scatter_vector(t, lo, hi):
             nc.vector.tensor_copy(out_win[t][:].indirect(listed(lo, hi)), dx[:, t, lo:hi])
 
-        def scatter_block(b):
-            lo, hi = b * P, (b + 1) * P
-            if b < BLOCKS // 2:
-                for t in range(4):
-                    scatter_scalar(t, lo, hi)
-            else:
-                scatter_scalar(0, lo, hi)
-                scatter_vector(1, lo, hi)
-
-        gathered = [gather(0), gather(1)]
-        pending = None
+        gather_x(0, C)
+        gather_x(C, S)
+        gather_dy(0, P)
+        gather_dy(P, C)
+        token_side(0)
+        token_side(1)
+        deal_words(w1t_first, 0, 1)
         for b in range(BLOCKS):
-            if b % 2 == 0:
-                deal_w1t(b // 2)
-            da = first_stage(b, *gathered[b])
-            if b + 2 < BLOCKS:
-                gathered.append(gather(b + 2))
-            if pending is not None:
-                second_stage(*pending)
-                scatter_block(pending[0])
-            pending = (b, da)
-        second_stage(*pending)
-        scatter_block(BLOCKS - 1)
-        scatter_scalar(2, S // 2, S)
-        scatter_vector(3, S // 2, S)
+            quantised = turn(b, gradient_side(b))
+            if b == 0:
+                deal_scales(0, 1)
+            second_stage(b, *quantised)
+            if b == 0:
+                for ahead in range(2, BLOCKS):
+                    token_side(ahead)
+                deal_words(w1t_rest, 1, E)
+            if b < 3:
+                for t in range(4):
+                    scatter_scalar(t, b * P, (b + 1) * P)
+            if b == 1:
+                gather_dy(C, 2 * C)
+                deal_scales(1, E)
+            if b == 3:
+                gather_dy(2 * C, S)
+        scatter_scalar(0, 3 * P, 5 * P)
+        scatter_scalar(2, 3 * P, 5 * P)
+        scatter_scalar(0, 5 * P, 6 * P)
+        scatter_scalar(2, 5 * P, 6 * P)
+        scatter_vector(1, 3 * P, 6 * P)
+        scatter_vector(3, 3 * P, 6 * P)
 
         rows = out_0.rearrange("(p t) n -> p t n", t=4)
         planes = held([P, 4, T], BF16, "planes")
         for t in range(4):
             nc.sync.dma_start(out=rows[:, t, :], in_=out_win[t][:])
-            if t == 2:
+            if "SVSV"[t] == "S":
                 nc.scalar.copy(out=planes[:, t, :], in_=out_win[t][:])
+            elif "SVSV"[t] == "G":
+                nc.gpsimd.tensor_scalar(planes[:, t, :], out_win[t][:], 1.0, 0.0, ALU.mult, ALU.add)
             else:
                 nc.vector.tensor_copy(out=planes[:, t, :], in_=out_win[t][:])
 

@@ -43,7 +43,8 @@ def tile_moe_rec_mlp_silu_kernel(
         w1_sc = held([P, E * H], U8, "w1_sc")
         w2_sc = held([P, E * 2 * H], U8, "w2_sc")
         w1t_sc_raw = held([P, E * K], U8, "w1t_sc_raw")
-        w1_all = held([P, E * 2 * H], U8, "w1_all")
+        w1_first = held([P, 2 * H], U8, "w1_first")
+        w1_rest = held([P, (E - 1) * 2 * H], U8, "w1_rest")
         w2_first = held([P, 2 * 2 * H], U8, "w2_first")
         w2_rest = held([P, (E - 1) * 2 * 2 * H], U8, "w2_rest")
         w1t_first = held([P, 2 * K], U8, "w1t_first")
@@ -77,12 +78,13 @@ def tile_moe_rec_mlp_silu_kernel(
         nc.sync.dma_start(offsets[:], offs)
         nc.sync.dma_start(out=x_win[:], in_=x_words[0].rearrange("p t d -> p (t d)").bitcast(I32))
         load_scales(xs_win, x_scales, 1)
+        load_words(w1_first, w1_w[0:1], 1)
         load_words(dy_win, dy_words.rearrange("s p t d -> s p (t d)"), 2)
-        load_words(w1_all, w1_w, E)
-        nc.sync.dma_start(out=g_rows[:], in_=gate.rearrange("r (b j) -> (r b) j", j=P)[0:P, :])
         load_scales(w1_sc, w1_scales.rearrange("e s b i -> (e s) b i"), E)
-        load_scales(dys_win, dy_scales, 2)
+        nc.sync.dma_start(out=g_rows[:], in_=gate.rearrange("r (b j) -> (r b) j", j=P)[0:P, :])
         load_words(w2_first, w2_w[0:2], 2)
+        load_scales(dys_win, dy_scales, 2)
+        load_words(w1_rest, w1_w[1:E], E - 1)
         load_scales(w2_sc, w2t_scales.rearrange("e s b i -> (e s) b i"), 2 * E)
         load_words(w1t_first, w1t_w[0:1], 1)
         load_scales(w1t_sc_raw, w1t_scales.rearrange("e s b i -> (e s) b i"), E)
@@ -96,7 +98,7 @@ def tile_moe_rec_mlp_silu_kernel(
 
         g_turned = psum.tile([P, 2, P], F32, name="turned")
         nc.tensor.transpose(g_turned[:, 0, :], g_rows[:], ident[:])
-        nc.scalar.activation(out=g_neg[:], in_=g_turned[:, 0, 0:BLOCKS], func=ACT.Copy, scale=-0.5)
+        nc.vector.tensor_scalar_mul(g_neg[:], g_turned[:, 0, 0:BLOCKS], -0.5)
 
         def expert_words(first, rest, e, width):
             if e == 0:
@@ -161,7 +163,7 @@ def tile_moe_rec_mlp_silu_kernel(
             a_ps = psum.tile([P, H], F32, name="a_ps")
             nc.tensor.matmul_mx(
                 out=a_ps[:], lhsT=x_g.bitcast(FP8X4), lhsT_scale=xs_g,
-                rhs=w1_all[:, e * 2 * H:(e + 1) * 2 * H].bitcast(FP4X4),
+                rhs=expert_words(w1_first, w1_rest, e, 2 * H).bitcast(FP4X4),
                 rhs_scale=w1_sc[:, e * H:(e + 1) * H], start=True, stop=True,
             )
             n = held([P, H], F32, f"n{b}")
@@ -169,7 +171,7 @@ def tile_moe_rec_mlp_silu_kernel(
             th = held([P, H], F32, f"th{b}")
             nc.scalar.activation(out=th[:], in_=a_ps[:], func=ACT.Tanh, scale=0.5)
             sg = held([P, H], F32, f"sg{b}")
-            nc.gpsimd.tensor_scalar(sg[:], th[:], g_neg[:, b:b + 1], g_neg[:, b:b + 1], ALU.mult, ALU.add)
+            nc.vector.tensor_scalar(sg[:], th[:], g_neg[:, b:b + 1], g_neg[:, b:b + 1], ALU.mult, ALU.add)
             n_of[b], sg_of[b] = n, sg
 
         def gradient_side(b):
@@ -248,11 +250,12 @@ def tile_moe_rec_mlp_silu_kernel(
                 deal_scales(1, E)
             if b == 3:
                 gather_dy(2 * C, S)
-        scatter_scalar(0, 3 * P, 5 * P)
-        scatter_scalar(2, 3 * P, 5 * P)
-        scatter_scalar(0, 5 * P, 6 * P)
-        scatter_scalar(2, 5 * P, 6 * P)
-        scatter_vector(1, 3 * P, 6 * P)
+        scatter_scalar(0, 3 * P, 4 * P)
+        scatter_scalar(2, 3 * P, 4 * P)
+        scatter_scalar(1, 3 * P, 4 * P)
+        scatter_scalar(0, 4 * P, 6 * P)
+        scatter_scalar(2, 4 * P, 6 * P)
+        scatter_vector(1, 4 * P, 6 * P)
         scatter_vector(3, 3 * P, 6 * P)
 
         rows = out_0.rearrange("(p t) n -> p t n", t=4)
@@ -268,7 +271,7 @@ def tile_moe_rec_mlp_silu_kernel(
 
         y_scales = held([P, T], U8, "y_scales")
         words_out = out_1[0].rearrange("p t d -> p (t d)").bitcast(I32)
-        for lo, hi, engine in ((0, 384, "scalar"), (384, 512, "vector"), (512, 1024, "vector")):
+        for lo, hi, engine in ((0, 512, "vector"), (512, 896, "scalar"), (896, 1024, "vector")):
             woven = held([P, (hi - lo) * 4], BF16, f"woven{lo}")
             src = planes[:, :, lo:hi].rearrange("p t n -> p n t")
             dst = woven[:].rearrange("p (n t) -> p n t", t=4)
@@ -280,6 +283,6 @@ def tile_moe_rec_mlp_silu_kernel(
             nc.vector.quantize_mx(out=y_codes[:].bitcast(FP8X4), scales=y_scales[:, lo:hi], in_=woven[:])
             nc.sync.dma_start(out=words_out[:, lo:hi], in_=y_codes[:])
         for q in range(4):
-            nc.sync.dma_start(
+            nc.scalar.dma_start(
                 out=out_2[0, 4 * q:4 * q + 4, :].bitcast(I32), in_=y_scales[32 * q:32 * q + 4, :].bitcast(I32)
             )

@@ -7,6 +7,8 @@ K, T, E, C, H, N = 512, 1024, 3, 256, 512, 1024
 S = E * C
 P = 128
 BLOCKS = S // P
+PACK = 4
+DY_PASSES = N // (P * PACK)
 FLOPS = 2 * S * (K * H + N * H + H * K)
 
 F32 = mybir.dt.float32
@@ -20,7 +22,23 @@ FP4X4 = mybir.dt.float4_e2m1fn_x4
 ALU = mybir.AluOpType
 ACT = mybir.ActivationFunctionType
 
-SLOT = {"w1t_perm0":"xs_g0","w1t_perm1":"da_t0","w1t_sc0":"v0","dy_g0_256":"dys_g0_0","dys_g0_256":"dys_g0_128","dy_g1_256":"dys_g1_0","dys_g1_256":"dys_g1_128","w1t_sc1":"da_t1","dy_g0_512":"scales1","dys_g0_512":"codes1","dy_g1_512":"v2","dys_g1_512":"da2","out_win3":"out_win3"}
+TAKES_OVER = {
+    "w1t_words0": "x_bytes0",
+    "w1t_bytes0": "v0",
+    "w1t_words1": "da_turned0",
+    "w1t_bytes1": "da_turned1",
+    "dy_words0_2": "dy_bytes0_0",
+    "dy_words1_2": "dy_bytes1_0",
+    "dy_bytes0_2": "dy_bytes0_1",
+    "dy_bytes1_2": "dy_bytes1_1",
+    "dy_words0_4": "da_bytes1",
+    "dy_bytes0_4": "da_words1",
+    "dy_words1_4": "v2",
+    "dy_bytes1_4": "da2",
+}
+
+VECTOR_EMPTIES_FROM = 3
+LAST_STEP = ((0, 512, "vector"), (512, 896, "scalar"), (896, 1024, "vector"))
 
 
 def tile_moe_rec_mlp_silu_kernel(
@@ -33,24 +51,24 @@ def tile_moe_rec_mlp_silu_kernel(
         psum = ctx.enter_context(tc.psum_pool(name="psum", bufs=2))
 
         def held(shape, dtype, name):
-            return keep.tile(shape, dtype, name=name, tag=SLOT.get(name, name), align_bytes=64)
+            return keep.tile(shape, dtype, name=name, tag=TAKES_OVER.get(name, name), align_bytes=64)
 
         offsets = keep.tile([P, S // 16], U16, name="offsets")
         x_win = held([P, T], I32, "x_win")
-        dy_win = held([P, 2 * T], I32, "dy_win")
+        dy_win = held([P, DY_PASSES * T], I32, "dy_win")
         xs_win = held([P, T], U8, "xs_win")
-        dys_win = held([P, 2 * T], U8, "dys_win")
+        dys_win = held([P, DY_PASSES * T], U8, "dys_win")
         w1_sc = held([P, E * H], U8, "w1_sc")
-        w2_sc = held([P, E * 2 * H], U8, "w2_sc")
+        w2_sc = held([P, E * DY_PASSES * H], U8, "w2_sc")
         w1t_sc_raw = held([P, E * K], U8, "w1t_sc_raw")
         w1_first = held([P, 2 * H], U8, "w1_first")
         w1_rest = held([P, (E - 1) * 2 * H], U8, "w1_rest")
-        w2_first = held([P, 2 * 2 * H], U8, "w2_first")
-        w2_rest = held([P, (E - 1) * 2 * 2 * H], U8, "w2_rest")
+        w2_first = held([P, DY_PASSES * 2 * H], U8, "w2_first")
+        w2_rest = held([P, (E - 1) * DY_PASSES * 2 * H], U8, "w2_rest")
         w1t_first = held([P, 2 * K], U8, "w1t_first")
         w1t_rest = held([P, (E - 1) * 2 * K], U8, "w1t_rest")
         g_rows = keep.tile([P, P], F32, name="g_rows")
-        g_neg = keep.tile([P, BLOCKS], F32, name="g_neg")
+        g_half = keep.tile([P, BLOCKS], F32, name="g_half")
         ident = keep.tile([P, P], F32, name="ident")
 
         for plane in (xs_win, dys_win):
@@ -58,111 +76,111 @@ def tile_moe_rec_mlp_silu_kernel(
         make_identity(nc, ident[:])
         nc.gpsimd.memset(w1t_sc_raw[:].bitcast(I32), 0)
 
-        def load_scales(plane, rows, n, quadrants=range(4), queue=nc.sync):
-            for q in quadrants:
-                queue.dma_start(
-                    out=plane[32 * q:32 * q + 4, :].bitcast(I32).rearrange("r (g w) -> r g w", g=n),
-                    in_=rows[:, 4 * q:4 * q + 4, :].bitcast(I32).rearrange("g r w -> r g w"),
+        def load_scales(plane, rows, first, last):
+            width = rows.shape[2]
+            for q in range(4):
+                nc.sync.dma_start(
+                    out=plane[32 * q:32 * q + 4, first * width:last * width]
+                    .bitcast(I32).rearrange("r (g w) -> r g w", g=last - first),
+                    in_=rows[first:last, 4 * q:4 * q + 4, :].bitcast(I32).rearrange("g r w -> r g w"),
                 )
 
-        def load_words(tile, words, n):
+        def load_words(tile, words):
             nc.sync.dma_start(
-                out=tile[:].bitcast(I32).rearrange("p (g w) -> p g w", g=n),
+                out=tile[:].bitcast(I32).rearrange("p (g w) -> p g w", g=words.shape[0]),
                 in_=words.bitcast(I32).rearrange("g p w -> p g w"),
             )
 
         w1_w = w1_words.rearrange("e s p c -> (e s) p c")
         w2_w = w2t_words.rearrange("e s p c -> (e s) p c")
         w1t_w = w1t_words.rearrange("e s p c -> (e s) p c")
+        w2_rows = w2t_scales.rearrange("e s b i -> (e s) b i")
 
         nc.sync.dma_start(offsets[:], offs)
         nc.sync.dma_start(out=x_win[:], in_=x_words[0].rearrange("p t d -> p (t d)").bitcast(I32))
-        load_scales(xs_win, x_scales, 1)
-        load_words(w1_first, w1_w[0:1], 1)
-        load_words(dy_win, dy_words.rearrange("s p t d -> s p (t d)"), 2)
-        load_scales(w1_sc, w1_scales.rearrange("e s b i -> (e s) b i"), E)
+        load_scales(xs_win, x_scales, 0, 1)
+        load_words(w1_first, w1_w[0:1])
+        load_words(dy_win, dy_words.rearrange("s p t d -> s p (t d)"))
+        load_scales(w1_sc, w1_scales.rearrange("e s b i -> (e s) b i"), 0, E)
         nc.sync.dma_start(out=g_rows[:], in_=gate.rearrange("r (b j) -> (r b) j", j=P)[0:P, :])
-        load_words(w2_first, w2_w[0:2], 2)
-        load_scales(dys_win, dy_scales, 2)
-        load_words(w1_rest, w1_w[1:E], E - 1)
-        load_scales(w2_sc, w2t_scales.rearrange("e s b i -> (e s) b i"), 2 * E)
-        load_words(w1t_first, w1t_w[0:1], 1)
-        load_scales(w1t_sc_raw, w1t_scales.rearrange("e s b i -> (e s) b i"), E)
-        load_words(w2_rest, w2_w[2:2 * E], 2 * (E - 1))
-        load_words(w1t_rest, w1t_w[1:E], E - 1)
+        load_words(w2_first, w2_w[0:DY_PASSES])
+        load_scales(dys_win, dy_scales, 0, DY_PASSES)
+        load_scales(w2_sc, w2_rows, 0, DY_PASSES)
+        load_words(w1_rest, w1_w[1:E])
+        load_words(w1t_first, w1t_w[0:1])
+        load_scales(w1t_sc_raw, w1t_scales.rearrange("e s b i -> (e s) b i"), 0, E)
+        load_words(w2_rest, w2_w[DY_PASSES:E * DY_PASSES])
+        load_scales(w2_sc, w2_rows, DY_PASSES, E * DY_PASSES)
+        load_words(w1t_rest, w1t_w[1:E])
 
-        out_win = [held([P, T], F32, f"out_win{t}") for t in range(4)]
-        for t in range(3):
-            nc.vector.memset(out_win[t][:], 0.0)
-        nc.gpsimd.memset(out_win[3][:], 0.0)
+        row_tile = [held([P, T], F32, f"row_tile{t}") for t in range(PACK)]
+        for t in range(PACK - 1):
+            nc.vector.memset(row_tile[t][:], 0.0)
+        nc.gpsimd.memset(row_tile[PACK - 1][:], 0.0)
 
         g_turned = psum.tile([P, 2, P], F32, name="turned")
         nc.tensor.transpose(g_turned[:, 0, :], g_rows[:], ident[:])
-        nc.vector.tensor_scalar_mul(g_neg[:], g_turned[:, 0, 0:BLOCKS], -0.5)
+        nc.vector.tensor_scalar_mul(g_half[:], g_turned[:, 0, 0:BLOCKS], -0.5)
 
-        def expert_words(first, rest, e, width):
+        def expert_words(own_tile, shared_tile, e, width):
             if e == 0:
-                return first[:, 0:width]
-            return rest[:, (e - 1) * width:e * width]
+                return own_tile[:, 0:width]
+            return shared_tile[:, (e - 1) * width:e * width]
 
-        def listed(lo, hi):
-            return offsets[:, lo // 16:hi // 16]
+        def listed(first, last):
+            return offsets[:, first * P // 16:last * P // 16]
 
-        w1t_perm, w1t_sc = {}, {}
+        w1t_dealt_words, w1t_dealt_bytes = {}, {}
 
-        def deal_words(words, first, last):
-            n = last - first
-            dealt = held([P, n * 2 * K], U8, f"w1t_perm{first}")
+        def deal_words(raw, first, last):
+            dealt = held([P, (last - first) * 2 * K], U8, f"w1t_words{first}")
             nc.scalar.copy(
-                out=dealt[:].bitcast(U16).rearrange("p (e t m) -> p e t m", e=n, t=4),
-                in_=words[:].bitcast(U16).rearrange("p (e m t) -> p e t m", e=n, t=4),
+                out=dealt[:].bitcast(U16).rearrange("p (e t m) -> p e t m", e=last - first, t=PACK),
+                in_=raw[:].bitcast(U16).rearrange("p (e m t) -> p e t m", e=last - first, t=PACK),
             )
             for e in range(first, last):
-                w1t_perm[e] = dealt[:, (e - first) * 2 * K:(e - first + 1) * 2 * K]
+                w1t_dealt_words[e] = dealt[:, (e - first) * 2 * K:(e - first + 1) * 2 * K]
 
-        def deal_scales(first, last):
-            n = last - first
-            dealt = held([P, n * K], U8, f"w1t_sc{first}")
+        def deal_bytes(first, last):
+            dealt = held([P, (last - first) * K], U8, f"w1t_bytes{first}")
             nc.vector.tensor_copy(
-                out=dealt[:].rearrange("p (e t m) -> p e t m", e=n, t=4),
-                in_=w1t_sc_raw[:, first * K:last * K].rearrange("p (e m t) -> p e t m", e=n, t=4),
+                out=dealt[:].rearrange("p (e t m) -> p e t m", e=last - first, t=PACK),
+                in_=w1t_sc_raw[:, first * K:last * K].rearrange("p (e m t) -> p e t m", e=last - first, t=PACK),
             )
             for e in range(first, last):
-                w1t_sc[e] = dealt[:, (e - first) * K:(e - first + 1) * K]
+                w1t_dealt_bytes[e] = dealt[:, (e - first) * K:(e - first + 1) * K]
 
         x_of, dy_of = {}, {}
 
-        def gather_x(lo, hi):
-            slots = listed(lo, hi)
-            x_g = held([P, hi - lo], U32, f"x_g{lo}")
-            xs_g = held([P, hi - lo], U8, f"xs_g{lo}")
-            nc.vector.tensor_copy(x_g[:], x_win[:].bitcast(U32).indirect(slots))
-            nc.vector.tensor_copy(xs_g[:], xs_win[:].indirect(slots))
-            for b in range(lo // P, hi // P):
-                cols = slice(b * P - lo, (b + 1) * P - lo)
-                x_of[b] = (x_g[:, cols], xs_g[:, cols])
+        def gather_x(first, last):
+            words = held([P, (last - first) * P], U32, f"x_words{first}")
+            scales = held([P, (last - first) * P], U8, f"x_bytes{first}")
+            nc.vector.tensor_copy(words[:], x_win[:].bitcast(U32).indirect(listed(first, last)))
+            nc.vector.tensor_copy(scales[:], xs_win[:].indirect(listed(first, last)))
+            for b in range(first, last):
+                cols = slice((b - first) * P, (b - first + 1) * P)
+                x_of[b] = (words[:, cols], scales[:, cols])
 
-        def gather_dy(lo, hi):
-            n = hi - lo
-            slots = listed(lo, hi)
-            dy_g = [held([P, n], U32, f"dy_g{s}_{lo}") for s in range(2)]
-            dys_g = [held([P, n], U8, f"dys_g{s}_{lo}") for s in range(2)]
-            for s in range(2):
-                nc.vector.tensor_copy(dy_g[s][:], dy_win[:, s * T:(s + 1) * T].bitcast(U32).indirect(slots))
-                nc.vector.tensor_copy(dys_g[s][:], dys_win[:, s * T:(s + 1) * T].indirect(slots))
-            for b in range(lo // P, hi // P):
-                cols = slice(b * P - lo, (b + 1) * P - lo)
-                dy_of[b] = ([g[:, cols] for g in dy_g], [g[:, cols] for g in dys_g])
+        def gather_dy(first, last):
+            words = [held([P, (last - first) * P], U32, f"dy_words{s}_{first}") for s in range(DY_PASSES)]
+            scales = [held([P, (last - first) * P], U8, f"dy_bytes{s}_{first}") for s in range(DY_PASSES)]
+            for s in range(DY_PASSES):
+                tokens = slice(s * T, (s + 1) * T)
+                nc.vector.tensor_copy(words[s][:], dy_win[:, tokens].bitcast(U32).indirect(listed(first, last)))
+                nc.vector.tensor_copy(scales[s][:], dys_win[:, tokens].indirect(listed(first, last)))
+            for b in range(first, last):
+                cols = slice((b - first) * P, (b - first + 1) * P)
+                dy_of[b] = ([w[:, cols] for w in words], [z[:, cols] for z in scales])
 
-        dx = held([P, 4, S], F32, "dx")
+        dx = held([P, PACK, S], F32, "dx")
         n_of, sg_of = {}, {}
 
         def token_side(b):
             e = b * P // C
-            x_g, xs_g = x_of[b]
+            words, scales = x_of[b]
             a_ps = psum.tile([P, H], F32, name="a_ps")
             nc.tensor.matmul_mx(
-                out=a_ps[:], lhsT=x_g.bitcast(FP8X4), lhsT_scale=xs_g,
+                out=a_ps[:], lhsT=words.bitcast(FP8X4), lhsT_scale=scales,
                 rhs=expert_words(w1_first, w1_rest, e, 2 * H).bitcast(FP4X4),
                 rhs_scale=w1_sc[:, e * H:(e + 1) * H], start=True, stop=True,
             )
@@ -171,19 +189,20 @@ def tile_moe_rec_mlp_silu_kernel(
             th = held([P, H], F32, f"th{b}")
             nc.scalar.activation(out=th[:], in_=a_ps[:], func=ACT.Tanh, scale=0.5)
             sg = held([P, H], F32, f"sg{b}")
-            nc.vector.tensor_scalar(sg[:], th[:], g_neg[:, b:b + 1], g_neg[:, b:b + 1], ALU.mult, ALU.add)
+            nc.gpsimd.tensor_scalar(sg[:], th[:], g_half[:, b:b + 1], g_half[:, b:b + 1], ALU.mult, ALU.add)
             n_of[b], sg_of[b] = n, sg
 
         def gradient_side(b):
             e = b * P // C
-            dy_g, dys_g = dy_of[b]
+            words, scales = dy_of[b]
             dh_ps = psum.tile([P, H], F32, name="dh_ps")
-            w2_e = expert_words(w2_first, w2_rest, e, 4 * H)
-            for s in range(2):
+            w2_e = expert_words(w2_first, w2_rest, e, DY_PASSES * 2 * H)
+            for s in range(DY_PASSES):
+                col = (DY_PASSES * e + s) * H
                 nc.tensor.matmul_mx(
-                    out=dh_ps[:], lhsT=dy_g[s].bitcast(FP8X4), lhsT_scale=dys_g[s],
+                    out=dh_ps[:], lhsT=words[s].bitcast(FP8X4), lhsT_scale=scales[s],
                     rhs=w2_e[:, s * 2 * H:(s + 1) * 2 * H].bitcast(FP4X4),
-                    rhs_scale=w2_sc[:, (2 * e + s) * H:(2 * e + s + 1) * H], start=(s == 0), stop=(s == 1),
+                    rhs_scale=w2_sc[:, col:col + H], start=(s == 0), stop=(s == DY_PASSES - 1),
                 )
             v = held([P, H], F32, f"v{b}")
             nc.vector.scalar_tensor_tensor(v[:], n_of[b][:], 1.0, dh_ps[:], ALU.subtract, ALU.mult)
@@ -191,98 +210,95 @@ def tile_moe_rec_mlp_silu_kernel(
             nc.vector.tensor_tensor(da[:], v[:], sg_of[b][:], ALU.mult)
             return da
 
-        def turn(b, da):
+        def turn_and_quantise(b, da):
             pairs = da[:].bitcast(F32)
             turned = psum.tile([P, 2, P], F32, name="turned")
             for h in range(2):
                 nc.tensor.transpose(turned[:, h, :], pairs[:, h:H // 2:2], ident[:])
-            da_t = held([P, P * 4], BF16, f"da_t{b}")
-            weave_pairs = nc.scalar.copy if b == 0 else nc.vector.tensor_copy
-            weave_pairs(
-                out=da_t[:].bitcast(F32).rearrange("p (j h) -> p j h", h=2),
+            da_turned = held([P, P * PACK], BF16, f"da_turned{b}")
+            copy_out = nc.scalar.copy if b == 0 else nc.vector.tensor_copy
+            copy_out(
+                out=da_turned[:].bitcast(F32).rearrange("p (j h) -> p j h", h=2),
                 in_=turned[:].rearrange("p h j -> p j h"),
             )
-            codes = held([P, P], U32, f"codes{b}")
-            scales = held([P, P], U8, f"scales{b}")
-            nc.vector.quantize_mx(out=codes[:].bitcast(FP8X4), scales=scales[:], in_=da_t[:])
-            return codes, scales
+            words = held([P, P], U32, f"da_words{b}")
+            scales = held([P, P], U8, f"da_bytes{b}")
+            nc.vector.quantize_mx(out=words[:].bitcast(FP8X4), scales=scales[:], in_=da_turned[:])
+            return words, scales
 
-        def second_stage(b, codes, scales):
+        def second_product(b, words, scales):
             e = b * P // C
-            cols = slice(b * P, (b + 1) * P)
-            dx_ps = psum.tile([P, 4, P], F32, name="dx_ps")
-            for t in range(4):
+            dx_ps = psum.tile([P, PACK, P], F32, name="dx_ps")
+            for t in range(PACK):
                 nc.tensor.matmul_mx(
-                    out=dx_ps[:, t, :], lhsT=w1t_perm[e][:, 2 * P * t:2 * P * (t + 1)].bitcast(FP4X4),
-                    lhsT_scale=w1t_sc[e][:, P * t:P * (t + 1)],
-                    rhs=codes[:].bitcast(FP8X4), rhs_scale=scales[:], start=True, stop=True,
+                    out=dx_ps[:, t, :], lhsT=w1t_dealt_words[e][:, 2 * P * t:2 * P * (t + 1)].bitcast(FP4X4),
+                    lhsT_scale=w1t_dealt_bytes[e][:, P * t:P * (t + 1)],
+                    rhs=words[:].bitcast(FP8X4), rhs_scale=scales[:], start=True, stop=True,
                 )
-            empty = nc.scalar.copy if b < 3 else nc.vector.tensor_copy
-            empty(out=dx[:, :, cols], in_=dx_ps[:])
+            copy_out = nc.scalar.copy if b < VECTOR_EMPTIES_FROM else nc.vector.tensor_copy
+            copy_out(out=dx[:, :, b * P:(b + 1) * P], in_=dx_ps[:])
 
-        def scatter_scalar(t, lo, hi):
-            nc.scalar.activation(out=out_win[t][:].indirect(listed(lo, hi)), in_=dx[:, t, lo:hi], func=ACT.Copy)
+        def scatter_scalar(t, first, last):
+            nc.scalar.activation(
+                out=row_tile[t][:].indirect(listed(first, last)), in_=dx[:, t, first * P:last * P], func=ACT.Copy
+            )
 
-        def scatter_vector(t, lo, hi):
-            nc.vector.tensor_copy(out_win[t][:].indirect(listed(lo, hi)), dx[:, t, lo:hi])
+        def scatter_vector(t, first, last):
+            nc.vector.tensor_copy(row_tile[t][:].indirect(listed(first, last)), dx[:, t, first * P:last * P])
 
-        gather_x(0, C)
-        gather_x(C, S)
-        gather_dy(0, P)
-        gather_dy(P, C)
+        gather_x(0, 2)
+        gather_x(2, BLOCKS)
+        gather_dy(0, 1)
+        gather_dy(1, 2)
         token_side(0)
         token_side(1)
         deal_words(w1t_first, 0, 1)
         for b in range(BLOCKS):
-            quantised = turn(b, gradient_side(b))
+            quantised = turn_and_quantise(b, gradient_side(b))
             if b == 0:
-                deal_scales(0, 1)
-            second_stage(b, *quantised)
+                deal_bytes(0, 1)
+            second_product(b, *quantised)
             if b == 0:
-                for ahead in range(2, BLOCKS):
-                    token_side(ahead)
+                for later in range(2, BLOCKS):
+                    token_side(later)
                 deal_words(w1t_rest, 1, E)
-            if b < 3:
-                for t in range(4):
-                    scatter_scalar(t, b * P, (b + 1) * P)
+            if b < 4:
+                for t in range(PACK if b < 2 else PACK - 1):
+                    scatter_scalar(t, b, b + 1)
             if b == 1:
-                gather_dy(C, 2 * C)
-                deal_scales(1, E)
+                gather_dy(2, 4)
+                deal_bytes(1, E)
             if b == 3:
-                gather_dy(2 * C, S)
-        scatter_scalar(0, 3 * P, 4 * P)
-        scatter_scalar(2, 3 * P, 4 * P)
-        scatter_scalar(1, 3 * P, 4 * P)
-        scatter_scalar(0, 4 * P, 6 * P)
-        scatter_scalar(2, 4 * P, 6 * P)
-        scatter_vector(1, 4 * P, 6 * P)
-        scatter_vector(3, 3 * P, 6 * P)
+                gather_dy(4, BLOCKS)
+        scatter_vector(3, 2, 4)
+        for t in range(PACK):
+            scatter = scatter_vector if t % 2 else scatter_scalar
+            scatter(t, 4, BLOCKS)
 
-        rows = out_0.rearrange("(p t) n -> p t n", t=4)
-        planes = held([P, 4, T], BF16, "planes")
-        for t in range(4):
-            nc.sync.dma_start(out=rows[:, t, :], in_=out_win[t][:])
-            if "SVSV"[t] == "S":
-                nc.scalar.copy(out=planes[:, t, :], in_=out_win[t][:])
-            elif "SVSV"[t] == "G":
-                nc.gpsimd.tensor_scalar(planes[:, t, :], out_win[t][:], 1.0, 0.0, ALU.mult, ALU.add)
+        out_rows = out_0.rearrange("(p t) n -> p t n", t=PACK)
+        rounded = held([P, PACK, T], BF16, "rounded")
+        for t in range(PACK):
+            nc.sync.dma_start(out=out_rows[:, t, :], in_=row_tile[t][:])
+            if t == 0:
+                nc.gpsimd.tensor_scalar(rounded[:, t, :], row_tile[t][:], 1.0, 0.0, ALU.mult, ALU.add)
+            elif t == 2:
+                nc.scalar.copy(out=rounded[:, t, :], in_=row_tile[t][:])
             else:
-                nc.vector.tensor_copy(out=planes[:, t, :], in_=out_win[t][:])
+                nc.vector.tensor_copy(out=rounded[:, t, :], in_=row_tile[t][:])
 
-        y_scales = held([P, T], U8, "y_scales")
+        y_bytes = held([P, T], U8, "y_bytes")
         words_out = out_1[0].rearrange("p t d -> p (t d)").bitcast(I32)
-        for lo, hi, engine in ((0, 512, "vector"), (512, 896, "scalar"), (896, 1024, "vector")):
-            woven = held([P, (hi - lo) * 4], BF16, f"woven{lo}")
-            src = planes[:, :, lo:hi].rearrange("p t n -> p n t")
-            dst = woven[:].rearrange("p (n t) -> p n t", t=4)
-            if engine == "scalar":
-                nc.scalar.copy(out=dst, in_=src)
-            else:
-                nc.vector.tensor_copy(out=dst, in_=src)
-            y_codes = held([P, hi - lo], I32, f"y_codes{lo}")
-            nc.vector.quantize_mx(out=y_codes[:].bitcast(FP8X4), scales=y_scales[:, lo:hi], in_=woven[:])
-            nc.sync.dma_start(out=words_out[:, lo:hi], in_=y_codes[:])
+        for lo, hi, engine in LAST_STEP:
+            side_by_side = held([P, (hi - lo) * PACK], BF16, f"side_by_side{lo}")
+            copy = nc.scalar.copy if engine == "scalar" else nc.vector.tensor_copy
+            copy(
+                out=side_by_side[:].rearrange("p (n t) -> p n t", t=PACK),
+                in_=rounded[:, :, lo:hi].rearrange("p t n -> p n t"),
+            )
+            y_words = held([P, hi - lo], I32, f"y_words{lo}")
+            nc.vector.quantize_mx(out=y_words[:].bitcast(FP8X4), scales=y_bytes[:, lo:hi], in_=side_by_side[:])
+            nc.sync.dma_start(out=words_out[:, lo:hi], in_=y_words[:])
         for q in range(4):
             nc.scalar.dma_start(
-                out=out_2[0, 4 * q:4 * q + 4, :].bitcast(I32), in_=y_scales[32 * q:32 * q + 4, :].bitcast(I32)
+                out=out_2[0, 4 * q:4 * q + 4, :].bitcast(I32), in_=y_bytes[32 * q:32 * q + 4, :].bitcast(I32)
             )

@@ -29,15 +29,12 @@ TAKES_OVER = {
     "w1t_bytes1": "da_turned1",
     "dy_words0_2": "dy_bytes0_0",
     "dy_words1_2": "dy_bytes1_0",
-    "dy_bytes0_2": "dy_bytes0_1",
-    "dy_bytes1_2": "dy_bytes1_1",
-    "dy_words0_4": "da_bytes1",
-    "dy_bytes0_4": "da_words1",
-    "dy_words1_4": "v2",
-    "dy_bytes1_4": "da2",
+    "dy_words0_4": "da1",
+    "dy_words1_4": "da_words0",
 }
 
 VECTOR_EMPTIES_FROM = 3
+VECTOR_SCATTERS_FROM = {1: 3, 3: 2}
 LAST_STEP = ((0, 512, "vector"), (512, 896, "scalar"), (896, 1024, "vector"))
 
 
@@ -58,6 +55,7 @@ def tile_moe_rec_mlp_silu_kernel(
         dy_win = held([P, DY_PASSES * T], I32, "dy_win")
         xs_win = held([P, T], U8, "xs_win")
         dys_win = held([P, DY_PASSES * T], U8, "dys_win")
+        both_win = held([P, T], U8, "both_win")
         w1_sc = held([P, E * H], U8, "w1_sc")
         w2_sc = held([P, E * DY_PASSES * H], U8, "w2_sc")
         w1t_sc_raw = held([P, E * K], U8, "w1t_sc_raw")
@@ -74,7 +72,8 @@ def tile_moe_rec_mlp_silu_kernel(
         for plane in (xs_win, dys_win):
             nc.gpsimd.memset(plane[:].bitcast(I32), 0)
         make_identity(nc, ident[:])
-        nc.gpsimd.memset(w1t_sc_raw[:].bitcast(I32), 0)
+        for plane in (w1t_sc_raw, both_win):
+            nc.gpsimd.memset(plane[:].bitcast(I32), 0)
 
         def load_scales(plane, rows, first, last):
             width = rows.shape[2]
@@ -107,6 +106,12 @@ def tile_moe_rec_mlp_silu_kernel(
         load_scales(dys_win, dy_scales, 0, DY_PASSES)
         load_scales(w2_sc, w2_rows, 0, DY_PASSES)
         load_words(w1_rest, w1_w[1:E])
+        for s in range(DY_PASSES):
+            for q in range(4):
+                nc.sync.dma_start(
+                    out=both_win[32 * q + 4 * s:32 * q + 4 * s + 4, :].bitcast(I32),
+                    in_=dy_scales[s, 4 * q:4 * q + 4, :].bitcast(I32),
+                )
         load_words(w1t_first, w1t_w[0:1])
         load_scales(w1t_sc_raw, w1t_scales.rearrange("e s b i -> (e s) b i"), 0, E)
         load_words(w2_rest, w2_w[DY_PASSES:E * DY_PASSES])
@@ -132,9 +137,9 @@ def tile_moe_rec_mlp_silu_kernel(
 
         w1t_dealt_words, w1t_dealt_bytes = {}, {}
 
-        def deal_words(raw, first, last):
+        def deal_words(copy, raw, first, last):
             dealt = held([P, (last - first) * 2 * K], U8, f"w1t_words{first}")
-            nc.scalar.copy(
+            copy(
                 out=dealt[:].bitcast(U16).rearrange("p (e t m) -> p e t m", e=last - first, t=PACK),
                 in_=raw[:].bitcast(U16).rearrange("p (e m t) -> p e t m", e=last - first, t=PACK),
             )
@@ -150,7 +155,10 @@ def tile_moe_rec_mlp_silu_kernel(
             for e in range(first, last):
                 w1t_dealt_bytes[e] = dealt[:, (e - first) * K:(e - first + 1) * K]
 
-        x_of, dy_of = {}, {}
+        x_of, dy_words_of, dy_bytes_of = {}, {}, {}
+
+        def block_columns(tile, first, b):
+            return tile[:, (b - first) * P:(b - first + 1) * P]
 
         def gather_x(first, last):
             words = held([P, (last - first) * P], U32, f"x_words{first}")
@@ -158,19 +166,36 @@ def tile_moe_rec_mlp_silu_kernel(
             nc.vector.tensor_copy(words[:], x_win[:].bitcast(U32).indirect(listed(first, last)))
             nc.vector.tensor_copy(scales[:], xs_win[:].indirect(listed(first, last)))
             for b in range(first, last):
-                cols = slice((b - first) * P, (b - first + 1) * P)
-                x_of[b] = (words[:, cols], scales[:, cols])
+                x_of[b] = (block_columns(words, first, b), block_columns(scales, first, b))
 
-        def gather_dy(first, last):
-            words = [held([P, (last - first) * P], U32, f"dy_words{s}_{first}") for s in range(DY_PASSES)]
-            scales = [held([P, (last - first) * P], U8, f"dy_bytes{s}_{first}") for s in range(DY_PASSES)]
+        def gather_dy(b):
+            words = [held([P, P], U32, f"dy_words{s}_{b}") for s in range(DY_PASSES)]
+            scales = [held([P, P], U8, f"dy_bytes{s}_{b}") for s in range(DY_PASSES)]
             for s in range(DY_PASSES):
                 tokens = slice(s * T, (s + 1) * T)
-                nc.vector.tensor_copy(words[s][:], dy_win[:, tokens].bitcast(U32).indirect(listed(first, last)))
-                nc.vector.tensor_copy(scales[s][:], dys_win[:, tokens].indirect(listed(first, last)))
+                nc.vector.tensor_copy(words[s][:], dy_win[:, tokens].bitcast(U32).indirect(listed(b, b + 1)))
+                nc.vector.tensor_copy(scales[s][:], dys_win[:, tokens].indirect(listed(b, b + 1)))
+            dy_words_of[b] = [w[:] for w in words]
+            dy_bytes_of[b] = [z[:] for z in scales]
+
+        def gather_dy_words(first, last):
+            words = [held([P, (last - first) * P], U32, f"dy_words{s}_{first}") for s in range(DY_PASSES)]
+            for s in range(DY_PASSES):
+                window = dy_win[:, s * T:(s + 1) * T].bitcast(U32)
+                nc.vector.tensor_copy(words[s][:], window.indirect(listed(first, last)))
             for b in range(first, last):
-                cols = slice((b - first) * P, (b - first + 1) * P)
-                dy_of[b] = ([w[:, cols] for w in words], [z[:, cols] for z in scales])
+                dy_words_of[b] = [block_columns(w, first, b) for w in words]
+
+        def gather_dy_bytes(first, last):
+            both = held([P, (last - first) * P], U8, "dy_bytes_both")
+            nc.vector.tensor_copy(both[:], both_win[:].indirect(listed(first, last)))
+            second = held([P, (last - first) * P], U8, "dy_bytes_second")
+            for q in range(4):
+                nc.sync.dma_start(
+                    out=second[32 * q:32 * q + 4, :].bitcast(I32), in_=both[32 * q + 4:32 * q + 8, :].bitcast(I32)
+                )
+            for b in range(first, last):
+                dy_bytes_of[b] = [block_columns(both, first, b), block_columns(second, first, b)]
 
         dx = held([P, PACK, S], F32, "dx")
         n_of, sg_of = {}, {}
@@ -194,7 +219,7 @@ def tile_moe_rec_mlp_silu_kernel(
 
         def gradient_side(b):
             e = b * P // C
-            words, scales = dy_of[b]
+            words, scales = dy_words_of[b], dy_bytes_of[b]
             dh_ps = psum.tile([P, H], F32, name="dh_ps")
             w2_e = expert_words(w2_first, w2_rest, e, DY_PASSES * 2 * H)
             for s in range(DY_PASSES):
@@ -248,11 +273,12 @@ def tile_moe_rec_mlp_silu_kernel(
 
         gather_x(0, 2)
         gather_x(2, BLOCKS)
-        gather_dy(0, 1)
-        gather_dy(1, 2)
+        gather_dy(0)
+        gather_dy(1)
         token_side(0)
         token_side(1)
-        deal_words(w1t_first, 0, 1)
+        deal_words(nc.scalar.copy, w1t_first, 0, 1)
+        last_expert = BLOCKS - 2
         for b in range(BLOCKS):
             quantised = turn_and_quantise(b, gradient_side(b))
             if b == 0:
@@ -261,19 +287,22 @@ def tile_moe_rec_mlp_silu_kernel(
             if b == 0:
                 for later in range(2, BLOCKS):
                     token_side(later)
-                deal_words(w1t_rest, 1, E)
-            if b < 4:
-                for t in range(PACK if b < 2 else PACK - 1):
-                    scatter_scalar(t, b, b + 1)
+                deal_words(nc.vector.tensor_copy, w1t_rest, 1, E)
+            if b < last_expert:
+                for t in range(PACK):
+                    if b < VECTOR_SCATTERS_FROM.get(t, BLOCKS):
+                        scatter_scalar(t, b, b + 1)
             if b == 1:
-                gather_dy(2, 4)
+                gather_dy_bytes(2, BLOCKS)
+                gather_dy_words(2, last_expert)
                 deal_bytes(1, E)
-            if b == 3:
-                gather_dy(4, BLOCKS)
-        scatter_vector(3, 2, 4)
-        for t in range(PACK):
-            scatter = scatter_vector if t % 2 else scatter_scalar
-            scatter(t, 4, BLOCKS)
+            if b == last_expert - 1:
+                gather_dy_words(last_expert, BLOCKS)
+        scatter_vector(3, VECTOR_SCATTERS_FROM[3], last_expert)
+        scatter_scalar(0, last_expert, BLOCKS)
+        scatter_vector(1, VECTOR_SCATTERS_FROM[1], BLOCKS)
+        scatter_scalar(2, last_expert, BLOCKS)
+        scatter_vector(3, last_expert, BLOCKS)
 
         out_rows = out_0.rearrange("(p t) n -> p t n", t=PACK)
         rounded = held([P, PACK, T], BF16, "rounded")

from contextlib import ExitStack

import concourse.mybir as mybir
from concourse.masks import make_identity

K, T, E, C, H, N = 512, 1024, 3, 256, 512, 1024
S = E * C
P = 128
BLOCKS = S // P
PACK = 4
DY_PASSES = N // (P * PACK)
FLOPS = 2 * S * (K * H + N * H + H * K)

F32 = mybir.dt.float32
BF16 = mybir.dt.bfloat16
I32 = mybir.dt.int32
U32 = mybir.dt.uint32
U16 = mybir.dt.uint16
U8 = mybir.dt.uint8
FP8X4 = mybir.dt.float8_e4m3fn_x4
FP4X4 = mybir.dt.float4_e2m1fn_x4
ALU = mybir.AluOpType
ACT = mybir.ActivationFunctionType

TAKES_OVER = {
    "w1t_words0": "x_bytes0",
    "w1t_bytes0": "v0",
    "w1t_words1": "da_turned0",
    "w1t_bytes1": "da_turned1",
    "dy_words0_2": "dy_bytes0_0",
    "dy_words1_2": "dy_bytes1_0",
    "dy_words0_4": "da1",
    "dy_words1_4": "da_words0",
}

VECTOR_EMPTIES_FROM = 3
VECTOR_SCATTERS_FROM = {1: 3, 3: 2}
LAST_STEP = ((0, 512, "vector"), (512, 896, "scalar"), (896, 1024, "vector"))


def tile_moe_rec_mlp_silu_kernel(
    tc, x_words, x_scales, dy_words, dy_scales, w1_words, w1_scales, w2t_words, w2t_scales,
    w1t_words, w1t_scales, gate, offs, out_0, out_1, out_2,
):
    nc = tc.nc
    with ExitStack() as ctx:
        keep = ctx.enter_context(tc.tile_pool(name="keep", bufs=1))
        psum = ctx.enter_context(tc.psum_pool(name="psum", bufs=2))

        def held(shape, dtype, name):
            return keep.tile(shape, dtype, name=name, tag=TAKES_OVER.get(name, name), align_bytes=64)

        offsets = keep.tile([P, S // 16], U16, name="offsets")
        x_win = held([P, T], I32, "x_win")
        dy_win = held([P, DY_PASSES * T], I32, "dy_win")
        xs_win = held([P, T], U8, "xs_win")
        dys_win = held([P, DY_PASSES * T], U8, "dys_win")
        both_win = held([P, T], U8, "both_win")
        w1_sc = held([P, E * H], U8, "w1_sc")
        w2_sc = held([P, E * DY_PASSES * H], U8, "w2_sc")
        w1t_sc_raw = held([P, E * K], U8, "w1t_sc_raw")
        w1_first = held([P, 2 * H], U8, "w1_first")
        w1_rest = held([P, (E - 1) * 2 * H], U8, "w1_rest")
        w2_first = held([P, DY_PASSES * 2 * H], U8, "w2_first")
        w2_rest = held([P, (E - 1) * DY_PASSES * 2 * H], U8, "w2_rest")
        w1t_first = held([P, 2 * K], U8, "w1t_first")
        w1t_rest = held([P, (E - 1) * 2 * K], U8, "w1t_rest")
        g_rows = keep.tile([P, P], F32, name="g_rows")
        g_half = keep.tile([P, BLOCKS], F32, name="g_half")
        ident = keep.tile([P, P], F32, name="ident")

        for plane in (xs_win, dys_win):
            nc.gpsimd.memset(plane[:].bitcast(I32), 0)
        make_identity(nc, ident[:])
        for plane in (w1t_sc_raw, both_win):
            nc.gpsimd.memset(plane[:].bitcast(I32), 0)

        def load_scales(plane, rows, first, last):
            width = rows.shape[2]
            for q in range(4):
                nc.sync.dma_start(
                    out=plane[32 * q:32 * q + 4, first * width:last * width]
                    .bitcast(I32).rearrange("r (g w) -> r g w", g=last - first),
                    in_=rows[first:last, 4 * q:4 * q + 4, :].bitcast(I32).rearrange("g r w -> r g w"),
                )

        def load_words(tile, words):
            nc.sync.dma_start(
                out=tile[:].bitcast(I32).rearrange("p (g w) -> p g w", g=words.shape[0]),
                in_=words.bitcast(I32).rearrange("g p w -> p g w"),
            )

        w1_w = w1_words.rearrange("e s p c -> (e s) p c")
        w2_w = w2t_words.rearrange("e s p c -> (e s) p c")
        w1t_w = w1t_words.rearrange("e s p c -> (e s) p c")
        w2_rows = w2t_scales.rearrange("e s b i -> (e s) b i")

        nc.sync.dma_start(offsets[:], offs)
        nc.sync.dma_start(out=x_win[:], in_=x_words[0].rearrange("p t d -> p (t d)").bitcast(I32))
        load_scales(xs_win, x_scales, 0, 1)
        load_words(w1_first, w1_w[0:1])
        load_words(dy_win, dy_words.rearrange("s p t d -> s p (t d)"))
        load_scales(w1_sc, w1_scales.rearrange("e s b i -> (e s) b i"), 0, E)
        nc.sync.dma_start(out=g_rows[:], in_=gate.rearrange("r (b j) -> (r b) j", j=P)[0:P, :])
        load_words(w2_first, w2_w[0:DY_PASSES])
        load_scales(dys_win, dy_scales, 0, DY_PASSES)
        load_scales(w2_sc, w2_rows, 0, DY_PASSES)
        load_words(w1_rest, w1_w[1:E])
        for s in range(DY_PASSES):
            for q in range(4):
                nc.sync.dma_start(
                    out=both_win[32 * q + 4 * s:32 * q + 4 * s + 4, :].bitcast(I32),
                    in_=dy_scales[s, 4 * q:4 * q + 4, :].bitcast(I32),
                )
        load_words(w1t_first, w1t_w[0:1])
        load_scales(w1t_sc_raw, w1t_scales.rearrange("e s b i -> (e s) b i"), 0, E)
        load_words(w2_rest, w2_w[DY_PASSES:E * DY_PASSES])
        load_scales(w2_sc, w2_rows, DY_PASSES, E * DY_PASSES)
        load_words(w1t_rest, w1t_w[1:E])

        row_tile = [held([P, T], F32, f"row_tile{t}") for t in range(PACK)]
        for t in range(PACK - 1):
            nc.vector.memset(row_tile[t][:], 0.0)
        nc.gpsimd.memset(row_tile[PACK - 1][:], 0.0)

        g_turned = psum.tile([P, 2, P], F32, name="turned")
        nc.tensor.transpose(g_turned[:, 0, :], g_rows[:], ident[:])
        nc.vector.tensor_scalar_mul(g_half[:], g_turned[:, 0, 0:BLOCKS], -0.5)

        def expert_words(own_tile, shared_tile, e, width):
            if e == 0:
                return own_tile[:, 0:width]
            return shared_tile[:, (e - 1) * width:e * width]

        def listed(first, last):
            return offsets[:, first * P // 16:last * P // 16]

        w1t_dealt_words, w1t_dealt_bytes = {}, {}

        def deal_words(copy, raw, first, last):
            dealt = held([P, (last - first) * 2 * K], U8, f"w1t_words{first}")
            copy(
                out=dealt[:].bitcast(U16).rearrange("p (e t m) -> p e t m", e=last - first, t=PACK),
                in_=raw[:].bitcast(U16).rearrange("p (e m t) -> p e t m", e=last - first, t=PACK),
            )
            for e in range(first, last):
                w1t_dealt_words[e] = dealt[:, (e - first) * 2 * K:(e - first + 1) * 2 * K]

        def deal_bytes(first, last):
            dealt = held([P, (last - first) * K], U8, f"w1t_bytes{first}")
            nc.vector.tensor_copy(
                out=dealt[:].rearrange("p (e t m) -> p e t m", e=last - first, t=PACK),
                in_=w1t_sc_raw[:, first * K:last * K].rearrange("p (e m t) -> p e t m", e=last - first, t=PACK),
            )
            for e in range(first, last):
                w1t_dealt_bytes[e] = dealt[:, (e - first) * K:(e - first + 1) * K]

        x_of, dy_words_of, dy_bytes_of = {}, {}, {}

        def block_columns(tile, first, b):
            return tile[:, (b - first) * P:(b - first + 1) * P]

        def gather_x(first, last):
            words = held([P, (last - first) * P], U32, f"x_words{first}")
            scales = held([P, (last - first) * P], U8, f"x_bytes{first}")
            nc.vector.tensor_copy(words[:], x_win[:].bitcast(U32).indirect(listed(first, last)))
            nc.vector.tensor_copy(scales[:], xs_win[:].indirect(listed(first, last)))
            for b in range(first, last):
                x_of[b] = (block_columns(words, first, b), block_columns(scales, first, b))

        def gather_dy(b):
            words = [held([P, P], U32, f"dy_words{s}_{b}") for s in range(DY_PASSES)]
            scales = [held([P, P], U8, f"dy_bytes{s}_{b}") for s in range(DY_PASSES)]
            for s in range(DY_PASSES):
                tokens = slice(s * T, (s + 1) * T)
                nc.vector.tensor_copy(words[s][:], dy_win[:, tokens].bitcast(U32).indirect(listed(b, b + 1)))
                nc.vector.tensor_copy(scales[s][:], dys_win[:, tokens].indirect(listed(b, b + 1)))
            dy_words_of[b] = [w[:] for w in words]
            dy_bytes_of[b] = [z[:] for z in scales]

        def gather_dy_words(first, last):
            words = [held([P, (last - first) * P], U32, f"dy_words{s}_{first}") for s in range(DY_PASSES)]
            for s in range(DY_PASSES):
                window = dy_win[:, s * T:(s + 1) * T].bitcast(U32)
                nc.vector.tensor_copy(words[s][:], window.indirect(listed(first, last)))
            for b in range(first, last):
                dy_words_of[b] = [block_columns(w, first, b) for w in words]

        def gather_dy_bytes(first, last):
            both = held([P, (last - first) * P], U8, "dy_bytes_both")
            nc.vector.tensor_copy(both[:], both_win[:].indirect(listed(first, last)))
            second = held([P, (last - first) * P], U8, "dy_bytes_second")
            for q in range(4):
                nc.sync.dma_start(
                    out=second[32 * q:32 * q + 4, :].bitcast(I32), in_=both[32 * q + 4:32 * q + 8, :].bitcast(I32)
                )
            for b in range(first, last):
                dy_bytes_of[b] = [block_columns(both, first, b), block_columns(second, first, b)]

        dx = held([P, PACK, S], F32, "dx")
        n_of, sg_of = {}, {}

        def token_side(b):
            e = b * P // C
            words, scales = x_of[b]
            a_ps = psum.tile([P, H], F32, name="a_ps")
            nc.tensor.matmul_mx(
                out=a_ps[:], lhsT=words.bitcast(FP8X4), lhsT_scale=scales,
                rhs=expert_words(w1_first, w1_rest, e, 2 * H).bitcast(FP4X4),
                rhs_scale=w1_sc[:, e * H:(e + 1) * H], start=True, stop=True,
            )
            n = held([P, H], F32, f"n{b}")
            nc.scalar.activation(out=n[:], in_=a_ps[:], func=ACT.Silu, scale=-1.0)
            th = held([P, H], F32, f"th{b}")
            nc.scalar.activation(out=th[:], in_=a_ps[:], func=ACT.Tanh, scale=0.5)
            sg = held([P, H], F32, f"sg{b}")
            nc.gpsimd.tensor_scalar(sg[:], th[:], g_half[:, b:b + 1], g_half[:, b:b + 1], ALU.mult, ALU.add)
            n_of[b], sg_of[b] = n, sg

        def gradient_side(b):
            e = b * P // C
            words, scales = dy_words_of[b], dy_bytes_of[b]
            dh_ps = psum.tile([P, H], F32, name="dh_ps")
            w2_e = expert_words(w2_first, w2_rest, e, DY_PASSES * 2 * H)
            for s in range(DY_PASSES):
                col = (DY_PASSES * e + s) * H
                nc.tensor.matmul_mx(
                    out=dh_ps[:], lhsT=words[s].bitcast(FP8X4), lhsT_scale=scales[s],
                    rhs=w2_e[:, s * 2 * H:(s + 1) * 2 * H].bitcast(FP4X4),
                    rhs_scale=w2_sc[:, col:col + H], start=(s == 0), stop=(s == DY_PASSES - 1),
                )
            v = held([P, H], F32, f"v{b}")
            nc.vector.scalar_tensor_tensor(v[:], n_of[b][:], 1.0, dh_ps[:], ALU.subtract, ALU.mult)
            da = held([P, H], BF16, f"da{b}")
            nc.vector.tensor_tensor(da[:], v[:], sg_of[b][:], ALU.mult)
            return da

        def turn_and_quantise(b, da):
            pairs = da[:].bitcast(F32)
            turned = psum.tile([P, 2, P], F32, name="turned")
            for h in range(2):
                nc.tensor.transpose(turned[:, h, :], pairs[:, h:H // 2:2], ident[:])
            da_turned = held([P, P * PACK], BF16, f"da_turned{b}")
            copy_out = nc.scalar.copy if b == 0 else nc.vector.tensor_copy
            copy_out(
                out=da_turned[:].bitcast(F32).rearrange("p (j h) -> p j h", h=2),
                in_=turned[:].rearrange("p h j -> p j h"),
            )
            words = held([P, P], U32, f"da_words{b}")
            scales = held([P, P], U8, f"da_bytes{b}")
            nc.vector.quantize_mx(out=words[:].bitcast(FP8X4), scales=scales[:], in_=da_turned[:])
            return words, scales

        def second_product(b, words, scales):
            e = b * P // C
            dx_ps = psum.tile([P, PACK, P], F32, name="dx_ps")
            for t in range(PACK):
                nc.tensor.matmul_mx(
                    out=dx_ps[:, t, :], lhsT=w1t_dealt_words[e][:, 2 * P * t:2 * P * (t + 1)].bitcast(FP4X4),
                    lhsT_scale=w1t_dealt_bytes[e][:, P * t:P * (t + 1)],
                    rhs=words[:].bitcast(FP8X4), rhs_scale=scales[:], start=True, stop=True,
                )
            copy_out = nc.scalar.copy if b < VECTOR_EMPTIES_FROM else nc.vector.tensor_copy
            copy_out(out=dx[:, :, b * P:(b + 1) * P], in_=dx_ps[:])

        def scatter_scalar(t, first, last):
            nc.scalar.activation(
                out=row_tile[t][:].indirect(listed(first, last)), in_=dx[:, t, first * P:last * P], func=ACT.Copy
            )

        def scatter_vector(t, first, last):
            nc.vector.tensor_copy(row_tile[t][:].indirect(listed(first, last)), dx[:, t, first * P:last * P])

        gather_x(0, 2)
        gather_x(2, BLOCKS)
        gather_dy(0)
        gather_dy(1)
        token_side(0)
        token_side(1)
        deal_words(nc.scalar.copy, w1t_first, 0, 1)
        last_expert = BLOCKS - 2
        for b in range(BLOCKS):
            quantised = turn_and_quantise(b, gradient_side(b))
            if b == 0:
                deal_bytes(0, 1)
            second_product(b, *quantised)
            if b == 0:
                for later in range(2, BLOCKS):
                    token_side(later)
                deal_words(nc.vector.tensor_copy, w1t_rest, 1, E)
            if b < last_expert:
                for t in range(PACK):
                    if b < VECTOR_SCATTERS_FROM.get(t, BLOCKS):
                        scatter_scalar(t, b, b + 1)
            if b == 1:
                gather_dy_bytes(2, BLOCKS)
                gather_dy_words(2, last_expert)
                deal_bytes(1, E)
            if b == last_expert - 1:
                gather_dy_words(last_expert, BLOCKS)
        scatter_vector(3, VECTOR_SCATTERS_FROM[3], last_expert)
        scatter_scalar(0, last_expert, BLOCKS)
        scatter_vector(1, VECTOR_SCATTERS_FROM[1], BLOCKS)
        scatter_scalar(2, last_expert, BLOCKS)
        scatter_vector(3, last_expert, BLOCKS)

        out_rows = out_0.rearrange("(p t) n -> p t n", t=PACK)
        rounded = held([P, PACK, T], BF16, "rounded")
        for t in range(PACK):
            nc.sync.dma_start(out=out_rows[:, t, :], in_=row_tile[t][:])
            if t == 0:
                nc.gpsimd.tensor_scalar(rounded[:, t, :], row_tile[t][:], 1.0, 0.0, ALU.mult, ALU.add)
            elif t == 2:
                nc.scalar.copy(out=rounded[:, t, :], in_=row_tile[t][:])
            else:
                nc.vector.tensor_copy(out=rounded[:, t, :], in_=row_tile[t][:])

        y_bytes = held([P, T], U8, "y_bytes")
        words_out = out_1[0].rearrange("p t d -> p (t d)").bitcast(I32)
        for lo, hi, engine in LAST_STEP:
            side_by_side = held([P, (hi - lo) * PACK], BF16, f"side_by_side{lo}")
            copy = nc.scalar.copy if engine == "scalar" else nc.vector.tensor_copy
            copy(
                out=side_by_side[:].rearrange("p (n t) -> p n t", t=PACK),
                in_=rounded[:, :, lo:hi].rearrange("p t n -> p n t"),
            )
            y_words = held([P, hi - lo], I32, f"y_words{lo}")
            nc.vector.quantize_mx(out=y_words[:].bitcast(FP8X4), scales=y_bytes[:, lo:hi], in_=side_by_side[:])
            nc.sync.dma_start(out=words_out[:, lo:hi], in_=y_words[:])
        for q in range(4):
            nc.scalar.dma_start(
                out=out_2[0, 4 * q:4 * q + 4, :].bitcast(I32), in_=y_bytes[32 * q:32 * q + 4, :].bitcast(I32)
            )
